import numpy as np
import ml_dtypes


def mxq(x, axis, fmt="e4m3"):
    dtype, down = {"e4m3": (ml_dtypes.float8_e4m3fn, 7), "e5m2": (ml_dtypes.float8_e5m2, 14)}[fmt]
    v = np.moveaxis(np.asarray(x, np.float32).astype(ml_dtypes.bfloat16).astype(np.float64), axis, -1)
    blocks = v.reshape(v.shape[:-1] + (-1, 32))
    amax = np.abs(blocks).max(-1, keepdims=True)
    byte = np.maximum(np.where(amax > 0, np.frexp(amax)[1] - 1 + 127, 0) - down, 1)
    scale = np.exp2(byte - 127.0)
    codes = (blocks / scale).astype(np.float32).astype(dtype).astype(np.float64)
    return np.moveaxis((codes * scale).reshape(v.shape), -1, axis)


WIDE = False


def mx_kscale(k):
    if not WIDE:
        return np.ones(k)
    levels = np.array([24, -24, 12, -12, 0])
    if k % 512:
        return np.exp2(np.random.permutation(np.resize(levels, k // 32))).repeat(32)
    a = np.empty((k // 512, 16))
    for p in range(k // 512):
        a[p, :8] = np.random.permutation(np.resize(levels, 8))
        for g in range(8):
            far = levels[np.abs(levels - a[p, g]) >= 10]
            a[p, g + 8] = far[np.random.randint(len(far))]
    return np.exp2(a.ravel()).repeat(32)


def f64(x):
    return np.asarray(x).astype(np.float64)


def striped8(idx):
    return np.concatenate([v.reshape(-1, 16).T for v in idx]).astype(np.uint16)


def unstriped8(offs):
    return np.stack([offs[16 * g:16 * g + 16].T.reshape(-1) for g in range(8)]).astype(np.int64)


E2M1 = np.array([0.0, 0.5, 1.0, 1.5, 2.0, 3.0, 4.0, 6.0, -0.0, -0.5, -1.0, -1.5, -2.0, -3.0, -4.0, -6.0])


def pack_weight(w, fmt):
    k, n = w.shape
    w = f64(np.asarray(w, np.float32).astype(ml_dtypes.bfloat16)).reshape(k // 32, 32, n)
    amax = np.abs(w).max(1)
    if fmt == "e4m3":
        byte = np.frexp(amax)[1] - 1 + 127 - 7
    else:
        mant, ex = np.frexp(amax / 6.0)
        byte = np.where(mant > 0.5, ex, ex - 1) + 127
    byte = np.clip(np.where(amax > 0, byte, 1), 1, 254)
    scaled = (w * np.exp2(127.0 - byte)[:, None, :]).reshape(k, n).astype(np.float32)
    by_word = np.ascontiguousarray(scaled.reshape(k // 512, 128, 4, n).transpose(0, 1, 3, 2))
    if fmt == "e4m3":
        words = by_word.astype(ml_dtypes.float8_e4m3fn).view(np.uint8)
    else:
        c = by_word.astype(ml_dtypes.float4_e2m1fn).view(np.uint8) & 0xF
        words = (c[..., 0::2] | (c[..., 1::2] << 4)).reshape(k // 512, 128, 2 * n)
    return np.ascontiguousarray(words), np.ascontiguousarray(byte.astype(np.uint8).reshape(k // 512, 16, n))


def unpack_weight(words, scales, fmt):
    g, _, n = scales.shape
    words = np.ascontiguousarray(words).reshape(g, 128, n, -1)
    if fmt == "e4m3":
        vals = words.view(ml_dtypes.float8_e4m3fn).astype(np.float64)
    else:
        nib = np.empty((g, 128, n, 4), np.uint8)
        nib[..., 0::2] = words & 0xF
        nib[..., 1::2] = words >> 4
        vals = E2M1[nib]
    vals = vals * np.repeat(np.exp2(scales.astype(np.float64) - 127.0), 8, axis=1)[..., None]
    return vals.transpose(0, 1, 3, 2).reshape(g * 512, n)


K, L, N, T, J = 1024, 512, 512, 2048, 1024


def setup_inputs():
    n = np.random.standard_normal
    s = mx_kscale(K)[:, None]
    s2 = mx_kscale(L)[:, None]
    p_wx = pack_weight(n((L, N)) / np.sqrt(L) / s2, "e2m1")
    return {
        "xT": (n((K, T)) * s).astype(np.float32),
        "wgt": np.repeat(np.random.uniform(0.5, 2.0, (8, J)), 16, axis=0).astype(np.float32),
        "wt": (n((K, N)) / np.sqrt(K) / s).astype(np.float32),
        "c": (n((L, J)) * s2).astype(np.float32),
        "wx_words": p_wx[0],
        "wx_scales": p_wx[1],
        "b": (0.3 * n(N)).astype(np.float32),
        "offs": striped8(np.stack([np.random.permutation(T)[:J] for _ in range(8)])),
    }


def reference(xT, wgt, wt, c, wx_words, wx_scales, b, offs):
    idx = unstriped8(offs)
    rows = np.arange(K)
    xg = f64(wgt)[rows // 4 % 128] * f64(xT)[rows[:, None], idx[rows % 512 // 64]]
    xT_ = mxq(xg, 0, "e4m3")
    wt_q_ = mxq(f64(wt), 0, "e4m3")
    wt_r_ = mxq(f64(wt) - wt_q_, 0, "e4m3")
    c_ = mxq(f64(c), 0, "e4m3")
    wx_ = unpack_weight(wx_words, wx_scales, "e2m1")
    y = wt_q_.T @ xT_ + wt_r_.T @ xT_ + wx_.T @ c_
    return y + f64(b)[:, None]

@@ -1,0 +1,207 @@
+from contextlib import ExitStack
+
+import concourse.mybir as mybir
+from concourse.masks import make_identity
+
+K, L, N, T, J = 1024, 512, 512, 2048, 1024
+FLOPS = 2 * N * J * (2 * K + L) + 2 * K * 512 * N
+
+F32 = mybir.dt.float32
+BF16 = mybir.dt.bfloat16
+I32 = mybir.dt.int32
+U32 = mybir.dt.uint32
+U16 = mybir.dt.uint16
+U8 = mybir.dt.uint8
+FP8X4 = mybir.dt.float8_e4m3fn_x4
+FP4X4 = mybir.dt.float4_e2m1fn_x4
+MULT = mybir.AluOpType.mult
+SUB = mybir.AluOpType.subtract
+ADD = mybir.AluOpType.add
+IDENT = mybir.ActivationFunctionType.Identity
+
+P = 128
+PACK = 4
+KP = P * PACK
+HALF = 256
+
+
+def tile_list_tier_bias_kernel(tc, xT, wgt, wt, c, wx_words, wx_scales, b, offs, out):
+    nc = tc.nc
+    with ExitStack() as ctx:
+        keep = ctx.enter_context(tc.tile_pool(name="keep", bufs=1))
+        psum = ctx.enter_context(tc.psum_pool(name="psum", bufs=1))
+
+        def woven_out(tile):
+            return tile[:].rearrange("p (g i t) -> p g t i", i=4, t=PACK)
+
+        def woven_in(planes):
+            return planes.rearrange("p t (g i) -> p g t i", i=4)
+
+        def quantize(name, woven, width):
+            codes = keep.tile([P, width], U32, name=name + "_codes", align_bytes=64)
+            scales = keep.tile([P, width], U8, name=name + "_scales", align_bytes=64)
+            nc.vector.quantize_mx(out=codes[:].bitcast(FP8X4), scales=scales[:], in_=woven[:])
+            return codes, scales
+
+        def weave_and_quantize(name, planes, width, copy):
+            woven = keep.tile([P, width * PACK], BF16, name=name + "_woven", align_bytes=64)
+            copy(out=woven_out(woven), in_=woven_in(planes))
+            return quantize(name, woven, width)
+
+        offsets = keep.tile([P, J // 16], U16, name="offsets")
+        late = keep.tile([P, PACK * 256], F32, name="late")
+        wgt_a = late[:, 128:640]
+        wgt_bc = keep.tile([P, 512], F32, name="wgt_bc")
+        x_planes = [[keep.tile([P, T], F32, name="x%d%d" % (a, t)) for t in range(PACK)] for a in range(2)]
+        w_raw = [[keep.tile([P, PACK, HALF], F32, name="w%d%d" % (a, h)) for h in range(2)] for a in range(2)]
+        c_raw = [keep.tile([P, PACK, 512], F32, name="c%d" % h) for h in range(2)]
+        wx_codes = keep.tile([P, 2 * N], U8, name="wx_codes", align_bytes=64)
+        wx_plane = keep.tile([P, N], U8, name="wx_plane", align_bytes=64)
+        bias = keep.tile([P, N // P], F32, name="bias")
+
+        x_view = xT.rearrange("(a p t) s -> a t p s", p=P, t=PACK)
+        w_view = wt.rearrange("(a p t) n -> a p t n", p=P, t=PACK)
+        c_view = c.rearrange("(p t) j -> p t j", t=PACK)
+
+        def load_x(a, t):
+            nc.sync.dma_start(out=x_planes[a][t][:], in_=x_view[a, t])
+
+        def load_w(a, h):
+            nc.sync.dma_start(out=w_raw[a][h][:], in_=w_view[a, :, :, h * HALF:(h + 1) * HALF])
+
+        def load_c(h):
+            nc.sync.dma_start(out=c_raw[h][:], in_=c_view[:, :, h * 512:(h + 1) * 512])
+
+        eye = keep.tile([P, P], BF16, name="eye")
+        make_identity(nc, eye[:])
+        nc.gpsimd.memset(wx_plane[:].bitcast(I32), 0)
+        for q in range(4):
+            nc.scalar.dma_start(out=wx_plane[32 * q:32 * q + 4, :].bitcast(I32), in_=wx_scales[0, 4 * q:4 * q + 4, :].bitcast(I32))
+        warm = keep.tile([P, 1], F32, name="warm")
+        nc.scalar.activation(out=warm[:], in_=eye[:, 0:1], func=IDENT, bias=0.0, scale=1.0)
+        eye_woven = keep.tile([P, KP * PACK], BF16, name="eye_woven", align_bytes=64)
+        nc.vector.memset(eye_woven[:], 0.0)
+        eye_view = eye_woven[:].rearrange("p (j m t) -> p j m t", j=PACK, t=PACK)
+        for j in range(PACK):
+            nc.vector.tensor_copy(out=eye_view[:, j, :, j], in_=eye[:])
+        eye_codes, eye_scales = quantize("eye", eye_woven, KP)
+
+        nc.sync.dma_start(offsets[:], offs)
+        load_w(0, 0)
+        nc.sync.dma_start(out=wgt_a, in_=wgt[:, 0:512])
+        load_x(0, 0)
+        nc.sync.dma_start(out=wgt_bc[:], in_=wgt[:, 512:1024])
+        load_w(0, 1)
+        load_x(0, 1)
+        load_w(1, 0)
+        load_x(0, 2)
+        load_w(1, 1)
+        load_x(0, 3)
+        load_c(0)
+        load_x(1, 0)
+        load_x(1, 1)
+        load_c(1)
+        load_x(1, 2)
+        load_x(1, 3)
+        nc.sync.dma_start(out=wx_codes[:].bitcast(I32), in_=wx_words[0].bitcast(I32))
+        with nc.allow_non_contiguous_dma(reason="one bias value a partition"):
+            nc.sync.dma_start(out=bias[:], in_=b.rearrange("(m p) -> p m", p=P))
+
+        wq = {}
+        wr = {}
+
+        def tiers(a, h):
+            name = "w%d%d" % (a, h)
+            wq[a, h] = weave_and_quantize(name + "q", w_raw[a][h][:], HALF, nc.scalar.copy)
+            codes, scales = wq[a, h]
+            left = keep.tile([P, HALF * PACK], BF16, name=name + "r_woven", align_bytes=64)
+            for u in range(2):
+                cols = slice(u * P, (u + 1) * P)
+                back = psum.tile([P, PACK, P], F32, name="back", tag="shared%d" % (2 * h + u))
+                for j in range(PACK):
+                    rows = slice(j * P, (j + 1) * P)
+                    nc.tensor.matmul_mx(out=back[:, j, :], lhsT=eye_codes[:, rows].bitcast(FP8X4), lhsT_scale=eye_scales[:, rows],
+                                        rhs=codes[:, cols].bitcast(FP8X4), rhs_scale=scales[:, cols], start=True, stop=True)
+                nc.vector.tensor_tensor(out=woven_out(left[:, u * KP:(u + 1) * KP]), in0=woven_in(w_raw[a][h][:, :, cols]),
+                                        in1=woven_in(back[:]), op=SUB)
+            wr[a, h] = quantize(name + "r", left, HALF)
+
+        def gather(dst, a, t, weights, j0, width):
+            nc.vector.tensor_tensor(dst, x_planes[a][t][:].indirect(offsets[:, j0 // 16:(j0 + width) // 16]), weights, MULT)
+
+        g_a = [keep.tile([P, PACK, 512], F32, name="ga%d" % a) for a in range(2)]
+        g_bc0 = keep.tile([P, PACK, 512], F32, name="gbc0")
+        g_b1 = keep.tile([P, PACK, 256], F32, name="gb1")
+        g_c1 = late[:].rearrange("p (t s) -> p t s", t=PACK)
+
+        tiers(0, 0)
+        for t in range(PACK):
+            gather(g_a[0][:, t, :], 0, t, wgt_a, 0, 512)
+            gather(g_bc0[:, t, :], 0, t, wgt_bc[:], 512, 512)
+            if t < 3:
+                tiers((t + 1) // 2, (t + 1) % 2)
+        xa0 = weave_and_quantize("xa0", g_a[0][:], 512, nc.scalar.copy)
+        xbc0 = weave_and_quantize("xbc0", g_bc0[:], 512, nc.scalar.copy)
+        ca = weave_and_quantize("ca", c_raw[0][:], 512, nc.scalar.copy)
+        cbc = weave_and_quantize("cbc", c_raw[1][:], 512, nc.scalar.copy)
+        for t in range(PACK):
+            gather(g_a[1][:, t, :], 1, t, wgt_a, 0, 512)
+            gather(g_b1[:, t, :], 1, t, wgt_bc[:, 0:256], 512, 256)
+        xa1 = weave_and_quantize("xa1", g_a[1][:], 512, nc.scalar.copy)
+        xb1 = weave_and_quantize("xb1", g_b1[:], 256, nc.scalar.copy)
+        for t in range(PACK):
+            gather(g_c1[:, t, :], 1, t, wgt_bc[:, 256:512], 768, 256)
+        xc1 = weave_and_quantize("xc1", g_c1, 256, nc.vector.tensor_copy)
+
+        def fp8_pass(dst, w, a, m, x, cols, start, stop):
+            w_codes, w_scales = w[a, m // 2]
+            n_cols = slice((m % 2) * P, (m % 2 + 1) * P)
+            nc.tensor.matmul_mx(out=dst, lhsT=w_codes[:, n_cols].bitcast(FP8X4), lhsT_scale=w_scales[:, n_cols],
+                                rhs=x[0][:, cols].bitcast(FP8X4), rhs_scale=x[1][:, cols], start=start, stop=stop)
+
+        def fp4_pass(dst, m, x, cols):
+            nc.tensor.matmul_mx(out=dst, lhsT=wx_codes[:, 2 * m * P:2 * (m + 1) * P].bitcast(FP4X4), lhsT_scale=wx_plane[:, m * P:(m + 1) * P],
+                                rhs=x[0][:, cols].bitcast(FP8X4), rhs_scale=x[1][:, cols], start=False, stop=False)
+
+        def add_bias_scalar(dst, src, m):
+            nc.scalar.activation(out=dst, in_=src, func=IDENT, bias=bias[:, m:m + 1], scale=1.0)
+
+        def add_bias_vector(dst, src, m):
+            nc.vector.tensor_scalar(out=dst, in0=src, scalar1=bias[:, m:m + 1], scalar2=None, op0=ADD)
+
+        out_view = out.rearrange("(m p) j -> p m j", p=P)
+        whole = slice(0, 512)
+        acc_a = [psum.tile([P, 512], F32, name="acc_a%d" % m) for m in range(4)]
+        acc_n = [[psum.tile([P, 2, 256], F32, name="acc_n", tag="shared%d" % (2 * s + u)) for u in range(2)] for s in range(2)]
+
+        for m in range(4):
+            fp8_pass(acc_a[m][:], wq, 0, m, xa0, whole, True, False)
+            fp8_pass(acc_a[m][:], wr, 0, m, xa0, whole, False, False)
+        for s in range(2):
+            cols = slice(s * 256, (s + 1) * 256)
+            for m in range(4):
+                fp8_pass(acc_n[s][m // 2][:, m % 2, :], wq, 0, m, xbc0, cols, m % 2 == 0, False)
+                fp8_pass(acc_n[s][m // 2][:, m % 2, :], wr, 0, m, xbc0, cols, False, False)
+        for m in range(4):
+            fp4_pass(acc_a[m][:], m, ca, whole)
+        for s in range(2):
+            for m in range(4):
+                for v in range(2):
+                    fp4_pass(acc_n[s][m // 2][:, m % 2, v * P:(v + 1) * P], m, cbc, slice(s * 256 + v * P, s * 256 + (v + 1) * P))
+        for m in range(4):
+            fp8_pass(acc_a[m][:], wq, 1, m, xa1, whole, False, False)
+            fp8_pass(acc_a[m][:], wr, 1, m, xa1, whole, False, True)
+            res = keep.tile([P, 512], F32, name="res_a%d" % m)
+            add_bias_scalar(res[:], acc_a[m][:], m)
+            nc.sync.dma_start(out=out_view[:, m, 0:512], in_=res[:])
+        for s, x in enumerate((xb1, xc1)):
+            for u in range(2):
+                for v in range(2):
+                    m = 2 * u + v
+                    fp8_pass(acc_n[s][u][:, v, :], wq, 1, m, x, slice(0, 256), False, False)
+                    fp8_pass(acc_n[s][u][:, v, :], wr, 1, m, x, slice(0, 256), False, v == 1)
+                res = keep.tile([P, 2, 256], F32, name="res_n%d%d" % (s, u))
+                add_bias = add_bias_vector if (s, u) == (1, 1) else add_bias_scalar
+                for v in range(2):
+                    add_bias(res[:, v, :], acc_n[s][u][:, v, :], 2 * u + v)
+                nc.sync.dma_start(out=out_view[:, 2 * u:2 * u + 2, 512 + s * 256:768 + s * 256], in_=res[:])

@@ -37,24 +37,27 @@ def tile_list_tier_bias_kernel(tc, xT, wgt, wt, c, wx_words, wx_scales, b, offs,
         def woven_in(planes):
             return planes.rearrange("p t (g i) -> p g t i", i=4)
 
-        def quantize(name, woven, width):
-            codes = keep.tile([P, width], U32, name=name + "_codes", align_bytes=64)
+        def quantize(name, woven, width, codes=None):
+            if codes is None:
+                codes = keep.tile([P, width], U32, name=name + "_codes", align_bytes=64)
             scales = keep.tile([P, width], U8, name=name + "_scales", align_bytes=64)
             nc.vector.quantize_mx(out=codes[:].bitcast(FP8X4), scales=scales[:], in_=woven[:])
             return codes, scales
 
-        def weave_and_quantize(name, planes, width, copy):
-            woven = keep.tile([P, width * PACK], BF16, name=name + "_woven", align_bytes=64)
+        def weave_and_quantize(name, planes, width, copy, codes=None, woven=None):
+            if woven is None:
+                woven = keep.tile([P, width * PACK], BF16, name=name + "_woven", align_bytes=64)
             copy(out=woven_out(woven), in_=woven_in(planes))
-            return quantize(name, woven, width)
+            return quantize(name, woven, width, codes)
 
         offsets = keep.tile([P, J // 16], U16, name="offsets")
-        late = keep.tile([P, PACK * 256], F32, name="late")
-        wgt_a = late[:, 128:640]
-        wgt_bc = keep.tile([P, 512], F32, name="wgt_bc")
-        x_planes = [[keep.tile([P, T], F32, name="x%d%d" % (a, t)) for t in range(PACK)] for a in range(2)]
-        w_raw = [[keep.tile([P, PACK, HALF], F32, name="w%d%d" % (a, h)) for h in range(2)] for a in range(2)]
-        c_raw = [keep.tile([P, PACK, 512], F32, name="c%d" % h) for h in range(2)]
+        wgt_hi = keep.tile([P, 512], F32, name="wgt_hi")
+        wgt_lo = keep.tile([P, 512], F32, name="wgt_lo")
+        x_planes = [[keep.tile([P, T], F32, name="x%d%d" % (a, t), align_bytes=64) for t in range(PACK)] for a in range(2)]
+        g0 = keep.tile([P, PACK, J], F32, name="g0")
+        w_raw = [[keep.tile([P, PACK, HALF], F32, name="w%d%d" % (a, h))[:] if (a, h) != (1, 1) else g0[:, :, 0:HALF] for h in range(2)] for a in range(2)]
+        stage = keep.tile([P, PACK * J], F32, name="stage", align_bytes=64)
+        c_raw = [stage[:, 2 * J:4 * J].rearrange("p (t s) -> p t s", t=PACK), keep.tile([P, PACK, 512], F32, name="c1")]
         wx_codes = keep.tile([P, 2 * N], U8, name="wx_codes", align_bytes=64)
         wx_plane = keep.tile([P, N], U8, name="wx_plane", align_bytes=64)
         bias = keep.tile([P, N // P], F32, name="bias")
@@ -75,44 +78,41 @@ def tile_list_tier_bias_kernel(tc, xT, wgt, wt, c, wx_words, wx_scales, b, offs,
         eye = keep.tile([P, P], BF16, name="eye")
         make_identity(nc, eye[:])
         nc.gpsimd.memset(wx_plane[:].bitcast(I32), 0)
-        for q in range(4):
-            nc.scalar.dma_start(out=wx_plane[32 * q:32 * q + 4, :].bitcast(I32), in_=wx_scales[0, 4 * q:4 * q + 4, :].bitcast(I32))
         warm = keep.tile([P, 1], F32, name="warm")
         nc.scalar.activation(out=warm[:], in_=eye[:, 0:1], func=IDENT, bias=0.0, scale=1.0)
-        eye_woven = keep.tile([P, KP * PACK], BF16, name="eye_woven", align_bytes=64)
+        eye_woven = keep.tile([P, PACK * (KP + 1)], BF16, name="eye_woven", align_bytes=64)
         nc.vector.memset(eye_woven[:], 0.0)
-        eye_view = eye_woven[:].rearrange("p (j m t) -> p j m t", j=PACK, t=PACK)
-        for j in range(PACK):
-            nc.vector.tensor_copy(out=eye_view[:, j, :, j], in_=eye[:])
-        eye_codes, eye_scales = quantize("eye", eye_woven, KP)
+        eye_view = eye_woven[:].rearrange("p (j r) -> p j r", j=PACK)
+        nc.vector.tensor_copy(out=eye_view[:, :, 0:KP:PACK], in_=eye[:].unsqueeze(1).to_broadcast([P, PACK, P]))
+        eye_codes, eye_scales = quantize("eye", eye_woven[:, 0:KP * PACK], KP)
 
         nc.sync.dma_start(offsets[:], offs)
-        load_w(0, 0)
-        nc.sync.dma_start(out=wgt_a, in_=wgt[:, 0:512])
-        load_x(0, 0)
-        nc.sync.dma_start(out=wgt_bc[:], in_=wgt[:, 512:1024])
-        load_w(0, 1)
-        load_x(0, 1)
-        load_w(1, 0)
-        load_x(0, 2)
-        load_w(1, 1)
-        load_x(0, 3)
-        load_c(0)
-        load_x(1, 0)
-        load_x(1, 1)
+        for a in range(2):
+            for h in range(2):
+                load_w(a, h)
         load_c(1)
-        load_x(1, 2)
-        load_x(1, 3)
+        nc.sync.dma_start(out=wgt_hi[:], in_=wgt[:, 512:1024])
+        load_x(0, 0)
+        nc.sync.dma_start(out=wgt_lo[:], in_=wgt[:, 0:512])
         nc.sync.dma_start(out=wx_codes[:].bitcast(I32), in_=wx_words[0].bitcast(I32))
+        for q in range(4):
+            nc.sync.dma_start(out=wx_plane[32 * q:32 * q + 4, :].bitcast(I32), in_=wx_scales[0, 4 * q:4 * q + 4, :].bitcast(I32))
+        load_x(0, 1)
+        load_x(0, 2)
+        load_c(0)
+        load_x(0, 3)
+        for t in range(PACK):
+            load_x(1, t)
         with nc.allow_non_contiguous_dma(reason="one bias value a partition"):
             nc.sync.dma_start(out=bias[:], in_=b.rearrange("(m p) -> p m", p=P))
 
+        wq_codes = keep.tile([P, 4 * HALF], U32, name="wq_codes", tag="eye_woven", align_bytes=64)
         wq = {}
         wr = {}
 
         def tiers(a, h):
             name = "w%d%d" % (a, h)
-            wq[a, h] = weave_and_quantize(name + "q", w_raw[a][h][:], HALF, nc.scalar.copy)
+            wq[a, h] = weave_and_quantize(name + "q", w_raw[a][h][:], HALF, nc.scalar.copy, wq_codes[:, (2 * a + h) * HALF:(2 * a + h + 1) * HALF])
             codes, scales = wq[a, h]
             left = keep.tile([P, HALF * PACK], BF16, name=name + "r_woven", align_bytes=64)
             for u in range(2):
@@ -126,32 +126,37 @@ def tile_list_tier_bias_kernel(tc, xT, wgt, wt, c, wx_words, wx_scales, b, offs,
                                         in1=woven_in(back[:]), op=SUB)
             wr[a, h] = quantize(name + "r", left, HALF)
 
-        def gather(dst, a, t, weights, j0, width):
-            nc.vector.tensor_tensor(dst, x_planes[a][t][:].indirect(offsets[:, j0 // 16:(j0 + width) // 16]), weights, MULT)
+        def gather(dst, a, t, j0, width):
+            nc.vector.tensor_tensor(dst, x_planes[a][t][:].indirect(offsets[:, j0 // 16:(j0 + width) // 16]), (wgt_hi if j0 >= 512 else wgt_lo)[:, j0 % 512:j0 % 512 + width], MULT)
 
-        g_a = [keep.tile([P, PACK, 512], F32, name="ga%d" % a) for a in range(2)]
-        g_bc0 = keep.tile([P, PACK, 512], F32, name="gbc0")
-        g_b1 = keep.tile([P, PACK, 256], F32, name="gb1")
-        g_c1 = late[:].rearrange("p (t s) -> p t s", t=PACK)
 
-        tiers(0, 0)
+        for a in range(2):
+            for h in range(2):
+                tiers(a, h)
+        c_hi = weave_and_quantize("chi", c_raw[1][:], 512, nc.scalar.copy)
         for t in range(PACK):
-            gather(g_a[0][:, t, :], 0, t, wgt_a, 0, 512)
-            gather(g_bc0[:, t, :], 0, t, wgt_bc[:], 512, 512)
-            if t < 3:
-                tiers((t + 1) // 2, (t + 1) % 2)
-        xa0 = weave_and_quantize("xa0", g_a[0][:], 512, nc.scalar.copy)
-        xbc0 = weave_and_quantize("xbc0", g_bc0[:], 512, nc.scalar.copy)
-        ca = weave_and_quantize("ca", c_raw[0][:], 512, nc.scalar.copy)
-        cbc = weave_and_quantize("cbc", c_raw[1][:], 512, nc.scalar.copy)
+            gather(g0[:, t, 512:1024], 0, t, 512, 512)
+            gather(g0[:, t, 0:512], 0, t, 0, 512)
+        c_lo_codes = keep.tile([P, 512], U32, name="clo_codes", tag="x02", align_bytes=64)
+        c_lo = weave_and_quantize("clo", c_raw[0][:], 512, nc.scalar.copy, codes=c_lo_codes, woven=stage[:, 0:J].bitcast(BF16))
+        x0_hi = weave_and_quantize("x0hi", g0[:, :, 512:1024], 512, nc.scalar.copy, woven=stage[:, 2 * J:3 * J].bitcast(BF16))
+        x0_lo = weave_and_quantize("x0lo", g0[:, :, 0:512], 512, nc.scalar.copy, woven=stage[:, 3 * J:4 * J].bitcast(BF16))
+        g_a1 = stage[:].rearrange("p (t s) -> p t s", t=PACK)[:, :, 0:512]
         for t in range(PACK):
-            gather(g_a[1][:, t, :], 1, t, wgt_a, 0, 512)
-            gather(g_b1[:, t, :], 1, t, wgt_bc[:, 0:256], 512, 256)
-        xa1 = weave_and_quantize("xa1", g_a[1][:], 512, nc.scalar.copy)
+            gather(g_a1[:, t, :], 1, t, 512, 512)
+        xa1 = weave_and_quantize("xa1", g_a1, 512, nc.scalar.copy)
+        g_b1 = keep.tile([P, PACK, 256], F32, name="gb1", tag="wgt_hi")
+        for t in range(PACK):
+            gather(g_b1[:, t, :], 1, t, 256, 256)
         xb1 = weave_and_quantize("xb1", g_b1[:], 256, nc.scalar.copy)
+        g_c1 = keep.tile([P, PACK, 128], F32, name="gc1", tag="xa1_woven", align_bytes=64)
         for t in range(PACK):
-            gather(g_c1[:, t, :], 1, t, wgt_bc[:, 256:512], 768, 256)
-        xc1 = weave_and_quantize("xc1", g_c1, 256, nc.vector.tensor_copy)
+            gather(g_c1[:, t, :], 1, t, 128, 128)
+        xc1 = weave_and_quantize("xc1", g_c1[:], 128, nc.scalar.copy)
+        g_d1 = keep.tile([P, PACK, 128], F32, name="gd1", tag="xb1_woven", align_bytes=64)
+        for t in range(PACK):
+            gather(g_d1[:, t, :], 1, t, 0, 128)
+        xd1 = weave_and_quantize("xd1", g_d1[:], 128, nc.vector.tensor_copy)
 
         def fp8_pass(dst, w, a, m, x, cols, start, stop):
             w_codes, w_scales = w[a, m // 2]
@@ -159,49 +164,43 @@ def tile_list_tier_bias_kernel(tc, xT, wgt, wt, c, wx_words, wx_scales, b, offs,
             nc.tensor.matmul_mx(out=dst, lhsT=w_codes[:, n_cols].bitcast(FP8X4), lhsT_scale=w_scales[:, n_cols],
                                 rhs=x[0][:, cols].bitcast(FP8X4), rhs_scale=x[1][:, cols], start=start, stop=stop)
 
-        def fp4_pass(dst, m, x, cols):
+        def fp4_pass(dst, m, x, cols, start):
             nc.tensor.matmul_mx(out=dst, lhsT=wx_codes[:, 2 * m * P:2 * (m + 1) * P].bitcast(FP4X4), lhsT_scale=wx_plane[:, m * P:(m + 1) * P],
-                                rhs=x[0][:, cols].bitcast(FP8X4), rhs_scale=x[1][:, cols], start=False, stop=False)
-
-        def add_bias_scalar(dst, src, m):
-            nc.scalar.activation(out=dst, in_=src, func=IDENT, bias=bias[:, m:m + 1], scale=1.0)
-
-        def add_bias_vector(dst, src, m):
-            nc.vector.tensor_scalar(out=dst, in0=src, scalar1=bias[:, m:m + 1], scalar2=None, op0=ADD)
+                                rhs=x[0][:, cols].bitcast(FP8X4), rhs_scale=x[1][:, cols], start=start, stop=False)
 
         out_view = out.rearrange("(m p) j -> p m j", p=P)
-        whole = slice(0, 512)
-        acc_a = [psum.tile([P, 512], F32, name="acc_a%d" % m) for m in range(4)]
-        acc_n = [[psum.tile([P, 2, 256], F32, name="acc_n", tag="shared%d" % (2 * s + u)) for u in range(2)] for s in range(2)]
+        chunks = [
+            (512, 512, x0_hi, c_hi, xa1, ["own0", "own1", "own2", "own3"]),
+            (256, 256, x0_lo, c_lo, xb1, ["shared0", "shared1"]),
+            (128, 128, x0_lo, c_lo, xc1, ["shared2"]),
+            (0, 128, x0_lo, c_lo, xd1, ["shared3"]),
+        ]
+        banks = [[psum.tile([P, 512 // width, width], F32, name="acc", tag=tag) for tag in tags] for j0, width, x0, cq, x1, tags in chunks]
 
-        for m in range(4):
-            fp8_pass(acc_a[m][:], wq, 0, m, xa0, whole, True, False)
-            fp8_pass(acc_a[m][:], wr, 0, m, xa0, whole, False, False)
-        for s in range(2):
-            cols = slice(s * 256, (s + 1) * 256)
+        for (j0, width, x0, cq, x1, tags), acc in zip(chunks, banks):
+            per = 512 // width
+            step = 512 if width == 512 else P
             for m in range(4):
-                fp8_pass(acc_n[s][m // 2][:, m % 2, :], wq, 0, m, xbc0, cols, m % 2 == 0, False)
-                fp8_pass(acc_n[s][m // 2][:, m % 2, :], wr, 0, m, xbc0, cols, False, False)
-        for m in range(4):
-            fp4_pass(acc_a[m][:], m, ca, whole)
-        for s in range(2):
+                for v in range(0, width, step):
+                    fp4_pass(acc[m // per][:, m % per, v:v + step], m, cq, slice(j0 % 512 + v, j0 % 512 + v + step), m % per == 0 and v == 0)
+        for (j0, width, x0, cq, x1, tags), acc in zip(chunks, banks):
+            per = 512 // width
+            cols = slice(j0 % 512, j0 % 512 + width)
             for m in range(4):
-                for v in range(2):
-                    fp4_pass(acc_n[s][m // 2][:, m % 2, v * P:(v + 1) * P], m, cbc, slice(s * 256 + v * P, s * 256 + (v + 1) * P))
-        for m in range(4):
-            fp8_pass(acc_a[m][:], wq, 1, m, xa1, whole, False, False)
-            fp8_pass(acc_a[m][:], wr, 1, m, xa1, whole, False, True)
-            res = keep.tile([P, 512], F32, name="res_a%d" % m)
-            add_bias_scalar(res[:], acc_a[m][:], m)
-            nc.sync.dma_start(out=out_view[:, m, 0:512], in_=res[:])
-        for s, x in enumerate((xb1, xc1)):
-            for u in range(2):
-                for v in range(2):
-                    m = 2 * u + v
-                    fp8_pass(acc_n[s][u][:, v, :], wq, 1, m, x, slice(0, 256), False, False)
-                    fp8_pass(acc_n[s][u][:, v, :], wr, 1, m, x, slice(0, 256), False, v == 1)
-                res = keep.tile([P, 2, 256], F32, name="res_n%d%d" % (s, u))
-                add_bias = add_bias_vector if (s, u) == (1, 1) else add_bias_scalar
-                for v in range(2):
-                    add_bias(res[:, v, :], acc_n[s][u][:, v, :], 2 * u + v)
-                nc.sync.dma_start(out=out_view[:, 2 * u:2 * u + 2, 512 + s * 256:768 + s * 256], in_=res[:])
+                fp8_pass(acc[m // per][:, m % per, :], wq, 0, m, x0, cols, False, False)
+                fp8_pass(acc[m // per][:, m % per, :], wr, 0, m, x0, cols, False, False)
+        for (j0, width, x0, cq, x1, tags), acc in zip(chunks, banks):
+            per = 512 // width
+            for u, bank in enumerate(acc):
+                for v in range(per):
+                    m = u * per + v
+                    fp8_pass(bank[:, v, :], wq, 1, m, x1, slice(0, width), False, False)
+                    fp8_pass(bank[:, v, :], wr, 1, m, x1, slice(0, width), False, v == per - 1)
+                res = keep.tile([P, per, width], F32, name="res_" + tags[u])
+                if tags[u] in ("shared1", "shared2", "shared3"):
+                    nc.vector.tensor_tensor(out=res[:], in0=bank[:], in1=bias[:, u * per:(u + 1) * per].unsqueeze(2).to_broadcast([P, per, width]), op=ADD)
+                else:
+                    for v in range(per):
+                        m = u * per + v
+                        nc.scalar.activation(out=res[:, v, :], in_=bank[:, v, :], func=IDENT, bias=bias[:, m:m + 1], scale=1.0)
+                nc.sync.dma_start(out=out_view[:, u * per:(u + 1) * per, j0:j0 + width], in_=res[:])

@@ -21,43 +21,56 @@ IDENT = mybir.ActivationFunctionType.Identity
 
 P = 128
 PACK = 4
-KP = P * PACK
-HALF = 256
+K_PASS = P * PACK
+BANK = 512
+BANKS = 8
+RUN = 4
+PIECE = 256
+PIECES = [(a, n0) for a in range(K // K_PASS) for n0 in range(0, N, PIECE)]
+PIECES_ON_VECTOR = (0, len(PIECES) - 1)
+J_HALF = J // 2
+WIDE, NARROW = 256, 128
+WIDE_CHUNKS = (768, 512, 256)
+NARROW_CHUNKS = (128, 0)
+BANKS_ON_SCALAR = 5
 
 
 def tile_list_tier_bias_kernel(tc, xT, wgt, wt, c, wx_words, wx_scales, b, offs, out):
     nc = tc.nc
     with ExitStack() as ctx:
         keep = ctx.enter_context(tc.tile_pool(name="keep", bufs=1))
+        stage = ctx.enter_context(tc.tile_pool(name="stage", bufs=2))
         psum = ctx.enter_context(tc.psum_pool(name="psum", bufs=1))
 
-        def woven_out(tile):
-            return tile[:].rearrange("p (g i t) -> p g t i", i=4, t=PACK)
+        def woven_walk(woven):
+            return woven.rearrange("p (g i t) -> p g t i", i=RUN, t=PACK)
 
-        def woven_in(planes):
-            return planes.rearrange("p t (g i) -> p g t i", i=4)
+        def planes_walk(planes):
+            return planes.rearrange("p t (g i) -> p g t i", i=RUN)
 
-        def quantize(name, woven, width, codes=None):
-            if codes is None:
-                codes = keep.tile([P, width], U32, name=name + "_codes", align_bytes=64)
+        def mx_tiles(name, width, codes_tag=""):
+            codes = keep.tile([P, width], U32, name=name + "_codes", tag=codes_tag, align_bytes=64)
             scales = keep.tile([P, width], U8, name=name + "_scales", align_bytes=64)
-            nc.vector.quantize_mx(out=codes[:].bitcast(FP8X4), scales=scales[:], in_=woven[:])
             return codes, scales
 
-        def weave_and_quantize(name, planes, width, copy, codes=None, woven=None):
-            if woven is None:
-                woven = keep.tile([P, width * PACK], BF16, name=name + "_woven", align_bytes=64)
-            copy(out=woven_out(woven), in_=woven_in(planes))
-            return quantize(name, woven, width, codes)
+        def quantize(operand, cols, woven):
+            nc.vector.quantize_mx(out=operand[0][:, cols].bitcast(FP8X4), scales=operand[1][:, cols], in_=woven)
+
+        def woven_tile(name, width):
+            return keep.tile([P, width * PACK], BF16, name=name + "_woven", align_bytes=64)[:]
+
+        def weave_and_quantize(name, planes, width, woven, copy):
+            copy(out=woven_walk(woven), in_=planes_walk(planes))
+            operand = mx_tiles(name, width)
+            quantize(operand, slice(0, width), woven)
+            return operand
 
         offsets = keep.tile([P, J // 16], U16, name="offsets")
-        wgt_hi = keep.tile([P, 512], F32, name="wgt_hi")
-        wgt_lo = keep.tile([P, 512], F32, name="wgt_lo")
-        x_planes = [[keep.tile([P, T], F32, name="x%d%d" % (a, t), align_bytes=64) for t in range(PACK)] for a in range(2)]
-        g0 = keep.tile([P, PACK, J], F32, name="g0")
-        w_raw = [[keep.tile([P, PACK, HALF], F32, name="w%d%d" % (a, h))[:] if (a, h) != (1, 1) else g0[:, :, 0:HALF] for h in range(2)] for a in range(2)]
-        stage = keep.tile([P, PACK * J], F32, name="stage", align_bytes=64)
-        c_raw = [stage[:, 2 * J:4 * J].rearrange("p (t s) -> p t s", t=PACK), keep.tile([P, PACK, 512], F32, name="c1")]
+        weights = keep.tile([P, J], F32, name="weights")
+        x_planes = [[keep.tile([P, T], F32, name="x%d%d" % (a, t)) for t in range(PACK)] for a in range(2)]
+        picked0 = keep.tile([P, PACK, J], F32, name="picked0")
+        w_raw = [picked0[:, :, 0:PIECE]] + [keep.tile([P, PACK, PIECE], F32, name="w%d_%d" % piece)[:] for piece in PIECES[1:]]
+        c_raw = [keep.tile([P, PACK, J_HALF], F32, name="c%d" % h) for h in range(2)]
         wx_codes = keep.tile([P, 2 * N], U8, name="wx_codes", align_bytes=64)
         wx_plane = keep.tile([P, N], U8, name="wx_plane", align_bytes=64)
         bias = keep.tile([P, N // P], F32, name="bias")
@@ -69,138 +82,174 @@ def tile_list_tier_bias_kernel(tc, xT, wgt, wt, c, wx_words, wx_scales, b, offs,
         def load_x(a, t):
             nc.sync.dma_start(out=x_planes[a][t][:], in_=x_view[a, t])
 
-        def load_w(a, h):
-            nc.sync.dma_start(out=w_raw[a][h][:], in_=w_view[a, :, :, h * HALF:(h + 1) * HALF])
+        def load_w(i):
+            a, n0 = PIECES[i]
+            nc.sync.dma_start(out=w_raw[i], in_=w_view[a, :, :, n0:n0 + PIECE])
 
         def load_c(h):
-            nc.sync.dma_start(out=c_raw[h][:], in_=c_view[:, :, h * 512:(h + 1) * 512])
+            nc.sync.dma_start(out=c_raw[h][:], in_=c_view[:, :, h * J_HALF:(h + 1) * J_HALF])
 
-        eye = keep.tile([P, P], BF16, name="eye")
+        eye = keep.tile([P, P], F32, name="eye")
         make_identity(nc, eye[:])
         nc.gpsimd.memset(wx_plane[:].bitcast(I32), 0)
-        warm = keep.tile([P, 1], F32, name="warm")
-        nc.scalar.activation(out=warm[:], in_=eye[:, 0:1], func=IDENT, bias=0.0, scale=1.0)
-        eye_woven = keep.tile([P, PACK * (KP + 1)], BF16, name="eye_woven", align_bytes=64)
+        eye_woven = keep.tile([P, PACK * (K_PASS + 1)], BF16, name="eye_woven", align_bytes=64)
         nc.vector.memset(eye_woven[:], 0.0)
-        eye_view = eye_woven[:].rearrange("p (j r) -> p j r", j=PACK)
-        nc.vector.tensor_copy(out=eye_view[:, :, 0:KP:PACK], in_=eye[:].unsqueeze(1).to_broadcast([P, PACK, P]))
-        eye_codes, eye_scales = quantize("eye", eye_woven[:, 0:KP * PACK], KP)
+        eye_rows = eye_woven[:].rearrange("p (j r) -> p j r", j=PACK)
+        nc.vector.tensor_copy(out=eye_rows[:, :, 0:K_PASS:PACK], in_=eye[:].unsqueeze(1).to_broadcast([P, PACK, P]))
+        eye_mx = mx_tiles("eye", K_PASS)
+        quantize(eye_mx, slice(0, K_PASS), eye_woven[:, 0:K_PASS * PACK])
 
         nc.sync.dma_start(offsets[:], offs)
-        for a in range(2):
-            for h in range(2):
-                load_w(a, h)
-        load_c(1)
-        nc.sync.dma_start(out=wgt_hi[:], in_=wgt[:, 512:1024])
+        load_w(0)
+        load_w(1)
+        nc.sync.dma_start(out=weights[:], in_=wgt)
         load_x(0, 0)
-        nc.sync.dma_start(out=wgt_lo[:], in_=wgt[:, 0:512])
+        load_x(0, 1)
+        load_w(2)
+        load_x(0, 2)
+        load_w(3)
+        load_x(0, 3)
+        load_x(1, 0)
+        load_x(1, 1)
+        load_c(1)
+        load_x(1, 2)
+        load_c(0)
+        load_x(1, 3)
         nc.sync.dma_start(out=wx_codes[:].bitcast(I32), in_=wx_words[0].bitcast(I32))
         for q in range(4):
             nc.sync.dma_start(out=wx_plane[32 * q:32 * q + 4, :].bitcast(I32), in_=wx_scales[0, 4 * q:4 * q + 4, :].bitcast(I32))
-        load_x(0, 1)
-        load_x(0, 2)
-        load_c(0)
-        load_x(0, 3)
-        for t in range(PACK):
-            load_x(1, t)
         with nc.allow_non_contiguous_dma(reason="one bias value a partition"):
             nc.sync.dma_start(out=bias[:], in_=b.rearrange("(m p) -> p m", p=P))
 
-        wq_codes = keep.tile([P, 4 * HALF], U32, name="wq_codes", tag="eye_woven", align_bytes=64)
-        wq = {}
-        wr = {}
+        wq = mx_tiles("wq", 2 * N, codes_tag="eye_woven")
+        wr = mx_tiles("wr", 2 * N)
+        left_woven = keep.tile([P, 2 * N * PACK], BF16, name="left_woven", align_bytes=64)
+        picked1 = keep.tile([P, PACK * J], F32, name="picked1", align_bytes=64)
+        scratch_banks = []
 
-        def tiers(a, h):
-            name = "w%d%d" % (a, h)
-            wq[a, h] = weave_and_quantize(name + "q", w_raw[a][h][:], HALF, nc.scalar.copy, wq_codes[:, (2 * a + h) * HALF:(2 * a + h + 1) * HALF])
-            codes, scales = wq[a, h]
-            left = keep.tile([P, HALF * PACK], BF16, name=name + "r_woven", align_bytes=64)
-            for u in range(2):
+        def scratch_bank(shape):
+            bank = psum.tile(shape, F32, name="scratch", tag="bank%d" % (len(scratch_banks) % BANKS))
+            scratch_banks.append(bank)
+            return bank
+
+        def dequantize(dst, t, cols):
+            rows = slice(t * P, (t + 1) * P)
+            nc.tensor.matmul_mx(out=dst, lhsT=eye_mx[0][:, rows].bitcast(FP8X4), lhsT_scale=eye_mx[1][:, rows],
+                                rhs=wq[0][:, cols].bitcast(FP8X4), rhs_scale=wq[1][:, cols], start=True, stop=True)
+
+        def left_on_vector(i, first):
+            for u in range(PIECE // P):
+                back = scratch_bank([P, PACK, P])
+                for t in range(PACK):
+                    dequantize(back[:, t, :], t, slice(first + u * P, first + (u + 1) * P))
+                nc.vector.tensor_tensor(out=woven_walk(left_woven[:, (first + u * P) * PACK:(first + (u + 1) * P) * PACK]),
+                                        in0=planes_walk(w_raw[i][:, :, u * P:(u + 1) * P]), in1=planes_walk(back[:]), op=SUB)
+
+        def left_on_tensor(i, first):
+            minus_q = stage.tile([P, PACK, PIECE], F32, name="minus_q")
+            for t0 in range(0, PACK, 2):
+                back = scratch_bank([P, 2, PIECE])
+                for t in range(t0, t0 + 2):
+                    dequantize(back[:, t - t0, :], t, slice(first, first + PIECE))
+                nc.scalar.activation(out=minus_q[:, t0:t0 + 2, :], in_=back[:], func=IDENT, bias=0.0, scale=-1.0)
+            start = 2 * J + (len(PIECES) - 1 - i) * 2 * PIECE
+            rounded_words = picked1[:, start:start + 2 * PIECE]
+            for u in range(PIECE // P):
                 cols = slice(u * P, (u + 1) * P)
-                back = psum.tile([P, PACK, P], F32, name="back", tag="shared%d" % (2 * h + u))
-                for j in range(PACK):
-                    rows = slice(j * P, (j + 1) * P)
-                    nc.tensor.matmul_mx(out=back[:, j, :], lhsT=eye_codes[:, rows].bitcast(FP8X4), lhsT_scale=eye_scales[:, rows],
-                                        rhs=codes[:, cols].bitcast(FP8X4), rhs_scale=scales[:, cols], start=True, stop=True)
-                nc.vector.tensor_tensor(out=woven_out(left[:, u * KP:(u + 1) * KP]), in0=woven_in(w_raw[a][h][:, :, cols]),
-                                        in1=woven_in(back[:]), op=SUB)
-            wr[a, h] = quantize(name + "r", left, HALF)
+                diff = scratch_bank([P, PACK, P])
+                for t in range(PACK):
+                    nc.tensor.matmul(diff[:, t, :], w_raw[i][:, t, cols], eye[:], start=True, stop=False, is_transpose=True)
+                    nc.tensor.matmul(diff[:, t, :], minus_q[:, t, cols], eye[:], start=False, stop=True, is_transpose=True)
+                rounded = rounded_words[:, u * 2 * P:(u + 1) * 2 * P].bitcast(BF16)
+                nc.scalar.copy(out=rounded.rearrange("n (h p e) -> n h p e", h=2, e=2), in_=diff[:].rearrange("n (h e) p -> n h p e", h=2))
+            pairs = scratch_bank([P, PIECE // P, 2, P])
+            for u in range(PIECE // P):
+                for h in range(2):
+                    nc.tensor.transpose(pairs[:, u, h, :], rounded_words[:, (2 * u + h) * P:(2 * u + h + 1) * P], eye[:])
+            dst = left_woven[:, first * PACK:(first + PIECE) * PACK].bitcast(F32)
+            nc.scalar.copy(out=dst.rearrange("p (u n h) -> p u n h", u=PIECE // P, h=2), in_=pairs[:].rearrange("p u h n -> p u n h"))
+
+        def tiers(i):
+            a, n0 = PIECES[i]
+            first = a * N + n0
+            woven = woven_tile("wq%d" % i, PIECE)
+            nc.scalar.copy(out=woven_walk(woven), in_=planes_walk(w_raw[i]))
+            quantize(wq, slice(first, first + PIECE), woven)
+            (left_on_vector if i in PIECES_ON_VECTOR else left_on_tensor)(i, first)
+            if n0 + PIECE == N:
+                quantize(wr, slice(a * N, (a + 1) * N), left_woven[:, a * N * PACK:(a + 1) * N * PACK])
 
         def gather(dst, a, t, j0, width):
-            nc.vector.tensor_tensor(dst, x_planes[a][t][:].indirect(offsets[:, j0 // 16:(j0 + width) // 16]), (wgt_hi if j0 >= 512 else wgt_lo)[:, j0 % 512:j0 % 512 + width], MULT)
+            nc.vector.tensor_tensor(dst, x_planes[a][t][:].indirect(offsets[:, j0 // 16:(j0 + width) // 16]), weights[:, j0:j0 + width], MULT)
 
+        tiers(0)
+        tiers(1)
+        gather(picked0[:, 0, :], 0, 0, 0, J)
+        gather(picked0[:, 1, :], 0, 1, 0, J)
+        tiers(2)
+        gather(picked0[:, 2, :], 0, 2, 0, J)
+        tiers(3)
+        gather(picked0[:, 3, :], 0, 3, 0, J)
+        x0_high = weave_and_quantize("x0_high", picked0[:, :, J_HALF:J], J_HALF, picked1[:, 2 * J:3 * J].bitcast(BF16), nc.scalar.copy)
+        x0_low = weave_and_quantize("x0_low", picked0[:, :, 0:J_HALF], J_HALF, picked1[:, 3 * J:4 * J].bitcast(BF16), nc.scalar.copy)
+        c_high = weave_and_quantize("c_high", c_raw[1][:], J_HALF, woven_tile("c_high", J_HALF), nc.scalar.copy)
+        c_low = weave_and_quantize("c_low", c_raw[0][:], J_HALF, woven_tile("c_low", J_HALF), nc.scalar.copy)
 
-        for a in range(2):
-            for h in range(2):
-                tiers(a, h)
-        c_hi = weave_and_quantize("chi", c_raw[1][:], 512, nc.scalar.copy)
-        for t in range(PACK):
-            gather(g0[:, t, 512:1024], 0, t, 512, 512)
-            gather(g0[:, t, 0:512], 0, t, 0, 512)
-        c_lo_codes = keep.tile([P, 512], U32, name="clo_codes", tag="x02", align_bytes=64)
-        c_lo = weave_and_quantize("clo", c_raw[0][:], 512, nc.scalar.copy, codes=c_lo_codes, woven=stage[:, 0:J].bitcast(BF16))
-        x0_hi = weave_and_quantize("x0hi", g0[:, :, 512:1024], 512, nc.scalar.copy, woven=stage[:, 2 * J:3 * J].bitcast(BF16))
-        x0_lo = weave_and_quantize("x0lo", g0[:, :, 0:512], 512, nc.scalar.copy, woven=stage[:, 3 * J:4 * J].bitcast(BF16))
-        g_a1 = stage[:].rearrange("p (t s) -> p t s", t=PACK)[:, :, 0:512]
-        for t in range(PACK):
-            gather(g_a1[:, t, :], 1, t, 512, 512)
-        xa1 = weave_and_quantize("xa1", g_a1, 512, nc.scalar.copy)
-        g_b1 = keep.tile([P, PACK, 256], F32, name="gb1", tag="wgt_hi")
-        for t in range(PACK):
-            gather(g_b1[:, t, :], 1, t, 256, 256)
-        xb1 = weave_and_quantize("xb1", g_b1[:], 256, nc.scalar.copy)
-        g_c1 = keep.tile([P, PACK, 128], F32, name="gc1", tag="xa1_woven", align_bytes=64)
-        for t in range(PACK):
-            gather(g_c1[:, t, :], 1, t, 128, 128)
-        xc1 = weave_and_quantize("xc1", g_c1[:], 128, nc.scalar.copy)
-        g_d1 = keep.tile([P, PACK, 128], F32, name="gd1", tag="xb1_woven", align_bytes=64)
-        for t in range(PACK):
-            gather(g_d1[:, t, :], 1, t, 0, 128)
-        xd1 = weave_and_quantize("xd1", g_d1[:], 128, nc.vector.tensor_copy)
+        planes1 = picked1[:].rearrange("p (t s) -> p t s", t=PACK)
+        wide_from = WIDE_CHUNKS[-1]
+        for t in range(PACK - 1):
+            gather(planes1[:, t, wide_from:J], 1, t, wide_from, J - wide_from)
+        for j0 in WIDE_CHUNKS:
+            gather(planes1[:, PACK - 1, j0:j0 + WIDE], 1, PACK - 1, j0, WIDE)
+        x1 = {}
+        for j0 in WIDE_CHUNKS:
+            name = "x1_%d" % j0
+            x1[j0] = weave_and_quantize(name, planes1[:, :, j0:j0 + WIDE], WIDE, woven_tile(name, WIDE), nc.scalar.copy)
+        behind = (WIDE_CHUNKS[0], WIDE_CHUNKS[-1])
+        for j0, wide_j0, copy in zip(NARROW_CHUNKS, behind, (nc.scalar.copy, nc.vector.tensor_copy)):
+            name = "x1_%d" % j0
+            picked = keep.tile([P, PACK, NARROW], F32, name=name + "_picked", tag="x1_%d_woven" % wide_j0, align_bytes=64)
+            for t in range(PACK):
+                gather(picked[:, t, :], 1, t, j0, NARROW)
+            x1[j0] = weave_and_quantize(name, picked[:], NARROW, woven_tile(name, NARROW), copy)
 
         def fp8_pass(dst, w, a, m, x, cols, start, stop):
-            w_codes, w_scales = w[a, m // 2]
-            n_cols = slice((m % 2) * P, (m % 2 + 1) * P)
-            nc.tensor.matmul_mx(out=dst, lhsT=w_codes[:, n_cols].bitcast(FP8X4), lhsT_scale=w_scales[:, n_cols],
+            n_cols = slice(a * N + m * P, a * N + (m + 1) * P)
+            nc.tensor.matmul_mx(out=dst, lhsT=w[0][:, n_cols].bitcast(FP8X4), lhsT_scale=w[1][:, n_cols],
                                 rhs=x[0][:, cols].bitcast(FP8X4), rhs_scale=x[1][:, cols], start=start, stop=stop)
 
-        def fp4_pass(dst, m, x, cols, start):
+        def fp4_pass(dst, m, x, cols):
             nc.tensor.matmul_mx(out=dst, lhsT=wx_codes[:, 2 * m * P:2 * (m + 1) * P].bitcast(FP4X4), lhsT_scale=wx_plane[:, m * P:(m + 1) * P],
-                                rhs=x[0][:, cols].bitcast(FP8X4), rhs_scale=x[1][:, cols], start=start, stop=False)
+                                rhs=x[0][:, cols].bitcast(FP8X4), rhs_scale=x[1][:, cols], start=False, stop=False)
 
+        tiles = N // P
+        chunks = [(j0, WIDE) for j0 in WIDE_CHUNKS] + [(j0, NARROW) for j0 in NARROW_CHUNKS]
+        sums = []
+        for j0, width in chunks:
+            for m0 in range(0, tiles, BANK // width):
+                sums.append((j0, width, m0, psum.tile([P, BANK // width, width], F32, name="acc", tag="bank%d" % len(sums))))
+
+        for j0, width, m0, bank in sums:
+            x0 = x0_high if j0 >= J_HALF else x0_low
+            cols = slice(j0 % J_HALF, j0 % J_HALF + width)
+            for v in range(BANK // width):
+                fp8_pass(bank[:, v, :], wq, 0, m0 + v, x0, cols, v == 0, False)
+                fp8_pass(bank[:, v, :], wr, 0, m0 + v, x0, cols, False, False)
+        for j0, width, m0, bank in sums:
+            c_mx = c_high if j0 >= J_HALF else c_low
+            for v in range(BANK // width):
+                for s in range(0, width, P):
+                    fp4_pass(bank[:, v, s:s + P], m0 + v, c_mx, slice(j0 % J_HALF + s, j0 % J_HALF + s + P))
         out_view = out.rearrange("(m p) j -> p m j", p=P)
-        chunks = [
-            (512, 512, x0_hi, c_hi, xa1, ["own0", "own1", "own2", "own3"]),
-            (256, 256, x0_lo, c_lo, xb1, ["shared0", "shared1"]),
-            (128, 128, x0_lo, c_lo, xc1, ["shared2"]),
-            (0, 128, x0_lo, c_lo, xd1, ["shared3"]),
-        ]
-        banks = [[psum.tile([P, 512 // width, width], F32, name="acc", tag=tag) for tag in tags] for j0, width, x0, cq, x1, tags in chunks]
-
-        for (j0, width, x0, cq, x1, tags), acc in zip(chunks, banks):
-            per = 512 // width
-            step = 512 if width == 512 else P
-            for m in range(4):
-                for v in range(0, width, step):
-                    fp4_pass(acc[m // per][:, m % per, v:v + step], m, cq, slice(j0 % 512 + v, j0 % 512 + v + step), m % per == 0 and v == 0)
-        for (j0, width, x0, cq, x1, tags), acc in zip(chunks, banks):
-            per = 512 // width
-            cols = slice(j0 % 512, j0 % 512 + width)
-            for m in range(4):
-                fp8_pass(acc[m // per][:, m % per, :], wq, 0, m, x0, cols, False, False)
-                fp8_pass(acc[m // per][:, m % per, :], wr, 0, m, x0, cols, False, False)
-        for (j0, width, x0, cq, x1, tags), acc in zip(chunks, banks):
-            per = 512 // width
-            for u, bank in enumerate(acc):
+        for number, (j0, width, m0, bank) in enumerate(sums):
+            per = BANK // width
+            for v in range(per):
+                fp8_pass(bank[:, v, :], wq, 1, m0 + v, x1[j0], slice(0, width), False, False)
+                fp8_pass(bank[:, v, :], wr, 1, m0 + v, x1[j0], slice(0, width), False, v == per - 1)
+            result = keep.tile([P, per, width], F32, name="result%d" % number)
+            if number < BANKS_ON_SCALAR:
                 for v in range(per):
-                    m = u * per + v
-                    fp8_pass(bank[:, v, :], wq, 1, m, x1, slice(0, width), False, False)
-                    fp8_pass(bank[:, v, :], wr, 1, m, x1, slice(0, width), False, v == per - 1)
-                res = keep.tile([P, per, width], F32, name="res_" + tags[u])
-                if tags[u] in ("shared1", "shared2", "shared3"):
-                    nc.vector.tensor_tensor(out=res[:], in0=bank[:], in1=bias[:, u * per:(u + 1) * per].unsqueeze(2).to_broadcast([P, per, width]), op=ADD)
-                else:
-                    for v in range(per):
-                        m = u * per + v
-                        nc.scalar.activation(out=res[:, v, :], in_=bank[:, v, :], func=IDENT, bias=bias[:, m:m + 1], scale=1.0)
-                nc.sync.dma_start(out=out_view[:, u * per:(u + 1) * per, j0:j0 + width], in_=res[:])
+                    nc.scalar.activation(out=result[:, v, :], in_=bank[:, v, :], func=IDENT, bias=bias[:, m0 + v:m0 + v + 1], scale=1.0)
+            else:
+                nc.vector.tensor_tensor(out=result[:], in0=bank[:], in1=bias[:, m0:m0 + per].unsqueeze(2).to_broadcast([P, per, width]), op=ADD)
+            nc.sync.dma_start(out=out_view[:, m0:m0 + per, j0:j0 + width], in_=result[:])

from contextlib import ExitStack

import concourse.mybir as mybir
from concourse.masks import make_identity

K, L, N, T, J = 1024, 512, 512, 2048, 1024
FLOPS = 2 * N * J * (2 * K + L) + 2 * K * 512 * N

F32 = mybir.dt.float32
BF16 = mybir.dt.bfloat16
I32 = mybir.dt.int32
U32 = mybir.dt.uint32
U16 = mybir.dt.uint16
U8 = mybir.dt.uint8
FP8X4 = mybir.dt.float8_e4m3fn_x4
FP4X4 = mybir.dt.float4_e2m1fn_x4
MULT = mybir.AluOpType.mult
SUB = mybir.AluOpType.subtract
ADD = mybir.AluOpType.add
IDENT = mybir.ActivationFunctionType.Identity

P = 128
PACK = 4
K_PASS = P * PACK
BANK = 512
BANKS = 8
RUN = 4
PIECE = 256
PIECES = [(a, n0) for a in range(K // K_PASS) for n0 in range(0, N, PIECE)]
PIECES_ON_VECTOR = (0, len(PIECES) - 1)
J_HALF = J // 2
WIDE, NARROW = 256, 128
WIDE_CHUNKS = (768, 512, 256)
NARROW_CHUNKS = (128, 0)
BANKS_ON_SCALAR = 5


def tile_list_tier_bias_kernel(tc, xT, wgt, wt, c, wx_words, wx_scales, b, offs, out):
    nc = tc.nc
    with ExitStack() as ctx:
        keep = ctx.enter_context(tc.tile_pool(name="keep", bufs=1))
        stage = ctx.enter_context(tc.tile_pool(name="stage", bufs=2))
        psum = ctx.enter_context(tc.psum_pool(name="psum", bufs=1))

        def woven_walk(woven):
            return woven.rearrange("p (g i t) -> p g t i", i=RUN, t=PACK)

        def planes_walk(planes):
            return planes.rearrange("p t (g i) -> p g t i", i=RUN)

        def mx_tiles(name, width, codes_tag=""):
            codes = keep.tile([P, width], U32, name=name + "_codes", tag=codes_tag, align_bytes=64)
            scales = keep.tile([P, width], U8, name=name + "_scales", align_bytes=64)
            return codes, scales

        def quantize(operand, cols, woven):
            nc.vector.quantize_mx(out=operand[0][:, cols].bitcast(FP8X4), scales=operand[1][:, cols], in_=woven)

        def woven_tile(name, width):
            return keep.tile([P, width * PACK], BF16, name=name + "_woven", align_bytes=64)[:]

        def weave_and_quantize(name, planes, width, woven, copy):
            copy(out=woven_walk(woven), in_=planes_walk(planes))
            operand = mx_tiles(name, width)
            quantize(operand, slice(0, width), woven)
            return operand

        offsets = keep.tile([P, J // 16], U16, name="offsets")
        weights = keep.tile([P, J], F32, name="weights")
        x_planes = [[keep.tile([P, T], F32, name="x%d%d" % (a, t)) for t in range(PACK)] for a in range(2)]
        picked0 = keep.tile([P, PACK, J], F32, name="picked0")
        w_raw = [picked0[:, :, 0:PIECE]] + [keep.tile([P, PACK, PIECE], F32, name="w%d_%d" % piece)[:] for piece in PIECES[1:]]
        c_raw = [keep.tile([P, PACK, J_HALF], F32, name="c%d" % h) for h in range(2)]
        wx_codes = keep.tile([P, 2 * N], U8, name="wx_codes", align_bytes=64)
        wx_plane = keep.tile([P, N], U8, name="wx_plane", align_bytes=64)
        bias = keep.tile([P, N // P], F32, name="bias")

        x_view = xT.rearrange("(a p t) s -> a t p s", p=P, t=PACK)
        w_view = wt.rearrange("(a p t) n -> a p t n", p=P, t=PACK)
        c_view = c.rearrange("(p t) j -> p t j", t=PACK)

        def load_x(a, t):
            nc.sync.dma_start(out=x_planes[a][t][:], in_=x_view[a, t])

        def load_w(i):
            a, n0 = PIECES[i]
            nc.sync.dma_start(out=w_raw[i], in_=w_view[a, :, :, n0:n0 + PIECE])

        def load_c(h):
            nc.sync.dma_start(out=c_raw[h][:], in_=c_view[:, :, h * J_HALF:(h + 1) * J_HALF])

        eye = keep.tile([P, P], F32, name="eye")
        make_identity(nc, eye[:])
        nc.gpsimd.memset(wx_plane[:].bitcast(I32), 0)
        eye_woven = keep.tile([P, PACK * (K_PASS + 1)], BF16, name="eye_woven", align_bytes=64)
        nc.vector.memset(eye_woven[:], 0.0)
        eye_rows = eye_woven[:].rearrange("p (j r) -> p j r", j=PACK)
        nc.vector.tensor_copy(out=eye_rows[:, :, 0:K_PASS:PACK], in_=eye[:].unsqueeze(1).to_broadcast([P, PACK, P]))
        eye_mx = mx_tiles("eye", K_PASS)
        quantize(eye_mx, slice(0, K_PASS), eye_woven[:, 0:K_PASS * PACK])

        nc.sync.dma_start(offsets[:], offs)
        load_w(0)
        load_w(1)
        nc.sync.dma_start(out=weights[:], in_=wgt)
        load_x(0, 0)
        load_x(0, 1)
        load_w(2)
        load_x(0, 2)
        load_w(3)
        load_x(0, 3)
        load_x(1, 0)
        load_x(1, 1)
        load_c(1)
        load_x(1, 2)
        load_c(0)
        load_x(1, 3)
        nc.sync.dma_start(out=wx_codes[:].bitcast(I32), in_=wx_words[0].bitcast(I32))
        for q in range(4):
            nc.sync.dma_start(out=wx_plane[32 * q:32 * q + 4, :].bitcast(I32), in_=wx_scales[0, 4 * q:4 * q + 4, :].bitcast(I32))
        with nc.allow_non_contiguous_dma(reason="one bias value a partition"):
            nc.sync.dma_start(out=bias[:], in_=b.rearrange("(m p) -> p m", p=P))

        wq = mx_tiles("wq", 2 * N, codes_tag="eye_woven")
        wr = mx_tiles("wr", 2 * N)
        left_woven = keep.tile([P, 2 * N * PACK], BF16, name="left_woven", align_bytes=64)
        picked1 = keep.tile([P, PACK * J], F32, name="picked1", align_bytes=64)
        scratch_banks = []

        def scratch_bank(shape):
            bank = psum.tile(shape, F32, name="scratch", tag="bank%d" % (len(scratch_banks) % BANKS))
            scratch_banks.append(bank)
            return bank

        def dequantize(dst, t, cols):
            rows = slice(t * P, (t + 1) * P)
            nc.tensor.matmul_mx(out=dst, lhsT=eye_mx[0][:, rows].bitcast(FP8X4), lhsT_scale=eye_mx[1][:, rows],
                                rhs=wq[0][:, cols].bitcast(FP8X4), rhs_scale=wq[1][:, cols], start=True, stop=True)

        def left_on_vector(i, first):
            for u in range(PIECE // P):
                back = scratch_bank([P, PACK, P])
                for t in range(PACK):
                    dequantize(back[:, t, :], t, slice(first + u * P, first + (u + 1) * P))
                nc.vector.tensor_tensor(out=woven_walk(left_woven[:, (first + u * P) * PACK:(first + (u + 1) * P) * PACK]),
                                        in0=planes_walk(w_raw[i][:, :, u * P:(u + 1) * P]), in1=planes_walk(back[:]), op=SUB)

        def left_on_tensor(i, first):
            minus_q = stage.tile([P, PACK, PIECE], F32, name="minus_q")
            for t0 in range(0, PACK, 2):
                back = scratch_bank([P, 2, PIECE])
                for t in range(t0, t0 + 2):
                    dequantize(back[:, t - t0, :], t, slice(first, first + PIECE))
                nc.scalar.activation(out=minus_q[:, t0:t0 + 2, :], in_=back[:], func=IDENT, bias=0.0, scale=-1.0)
            start = 2 * J + (len(PIECES) - 1 - i) * 2 * PIECE
            rounded_words = picked1[:, start:start + 2 * PIECE]
            for u in range(PIECE // P):
                cols = slice(u * P, (u + 1) * P)
                diff = scratch_bank([P, PACK, P])
                for t in range(PACK):
                    nc.tensor.matmul(diff[:, t, :], w_raw[i][:, t, cols], eye[:], start=True, stop=False, is_transpose=True)
                    nc.tensor.matmul(diff[:, t, :], minus_q[:, t, cols], eye[:], start=False, stop=True, is_transpose=True)
                rounded = rounded_words[:, u * 2 * P:(u + 1) * 2 * P].bitcast(BF16)
                nc.scalar.copy(out=rounded.rearrange("n (h p e) -> n h p e", h=2, e=2), in_=diff[:].rearrange("n (h e) p -> n h p e", h=2))
            pairs = scratch_bank([P, PIECE // P, 2, P])
            for u in range(PIECE // P):
                for h in range(2):
                    nc.tensor.transpose(pairs[:, u, h, :], rounded_words[:, (2 * u + h) * P:(2 * u + h + 1) * P], eye[:])
            dst = left_woven[:, first * PACK:(first + PIECE) * PACK].bitcast(F32)
            nc.scalar.copy(out=dst.rearrange("p (u n h) -> p u n h", u=PIECE // P, h=2), in_=pairs[:].rearrange("p u h n -> p u n h"))

        def tiers(i):
            a, n0 = PIECES[i]
            first = a * N + n0
            woven = woven_tile("wq%d" % i, PIECE)
            nc.scalar.copy(out=woven_walk(woven), in_=planes_walk(w_raw[i]))
            quantize(wq, slice(first, first + PIECE), woven)
            (left_on_vector if i in PIECES_ON_VECTOR else left_on_tensor)(i, first)
            if n0 + PIECE == N:
                quantize(wr, slice(a * N, (a + 1) * N), left_woven[:, a * N * PACK:(a + 1) * N * PACK])

        def gather(dst, a, t, j0, width):
            nc.vector.tensor_tensor(dst, x_planes[a][t][:].indirect(offsets[:, j0 // 16:(j0 + width) // 16]), weights[:, j0:j0 + width], MULT)

        tiers(0)
        tiers(1)
        gather(picked0[:, 0, :], 0, 0, 0, J)
        gather(picked0[:, 1, :], 0, 1, 0, J)
        tiers(2)
        gather(picked0[:, 2, :], 0, 2, 0, J)
        tiers(3)
        gather(picked0[:, 3, :], 0, 3, 0, J)
        x0_high = weave_and_quantize("x0_high", picked0[:, :, J_HALF:J], J_HALF, picked1[:, 2 * J:3 * J].bitcast(BF16), nc.scalar.copy)
        x0_low = weave_and_quantize("x0_low", picked0[:, :, 0:J_HALF], J_HALF, picked1[:, 3 * J:4 * J].bitcast(BF16), nc.scalar.copy)
        c_high = weave_and_quantize("c_high", c_raw[1][:], J_HALF, woven_tile("c_high", J_HALF), nc.scalar.copy)
        c_low = weave_and_quantize("c_low", c_raw[0][:], J_HALF, woven_tile("c_low", J_HALF), nc.scalar.copy)

        planes1 = picked1[:].rearrange("p (t s) -> p t s", t=PACK)
        wide_from = WIDE_CHUNKS[-1]
        for t in range(PACK - 1):
            gather(planes1[:, t, wide_from:J], 1, t, wide_from, J - wide_from)
        for j0 in WIDE_CHUNKS:
            gather(planes1[:, PACK - 1, j0:j0 + WIDE], 1, PACK - 1, j0, WIDE)
        x1 = {}
        for j0 in WIDE_CHUNKS:
            name = "x1_%d" % j0
            x1[j0] = weave_and_quantize(name, planes1[:, :, j0:j0 + WIDE], WIDE, woven_tile(name, WIDE), nc.scalar.copy)
        behind = (WIDE_CHUNKS[0], WIDE_CHUNKS[-1])
        for j0, wide_j0, copy in zip(NARROW_CHUNKS, behind, (nc.scalar.copy, nc.vector.tensor_copy)):
            name = "x1_%d" % j0
            picked = keep.tile([P, PACK, NARROW], F32, name=name + "_picked", tag="x1_%d_woven" % wide_j0, align_bytes=64)
            for t in range(PACK):
                gather(picked[:, t, :], 1, t, j0, NARROW)
            x1[j0] = weave_and_quantize(name, picked[:], NARROW, woven_tile(name, NARROW), copy)

        def fp8_pass(dst, w, a, m, x, cols, start, stop):
            n_cols = slice(a * N + m * P, a * N + (m + 1) * P)
            nc.tensor.matmul_mx(out=dst, lhsT=w[0][:, n_cols].bitcast(FP8X4), lhsT_scale=w[1][:, n_cols],
                                rhs=x[0][:, cols].bitcast(FP8X4), rhs_scale=x[1][:, cols], start=start, stop=stop)

        def fp4_pass(dst, m, x, cols):
            nc.tensor.matmul_mx(out=dst, lhsT=wx_codes[:, 2 * m * P:2 * (m + 1) * P].bitcast(FP4X4), lhsT_scale=wx_plane[:, m * P:(m + 1) * P],
                                rhs=x[0][:, cols].bitcast(FP8X4), rhs_scale=x[1][:, cols], start=False, stop=False)

        tiles = N // P
        chunks = [(j0, WIDE) for j0 in WIDE_CHUNKS] + [(j0, NARROW) for j0 in NARROW_CHUNKS]
        sums = []
        for j0, width in chunks:
            for m0 in range(0, tiles, BANK // width):
                sums.append((j0, width, m0, psum.tile([P, BANK // width, width], F32, name="acc", tag="bank%d" % len(sums))))

        for j0, width, m0, bank in sums:
            x0 = x0_high if j0 >= J_HALF else x0_low
            cols = slice(j0 % J_HALF, j0 % J_HALF + width)
            for v in range(BANK // width):
                fp8_pass(bank[:, v, :], wq, 0, m0 + v, x0, cols, v == 0, False)
                fp8_pass(bank[:, v, :], wr, 0, m0 + v, x0, cols, False, False)
        for j0, width, m0, bank in sums:
            c_mx = c_high if j0 >= J_HALF else c_low
            for v in range(BANK // width):
                for s in range(0, width, P):
                    fp4_pass(bank[:, v, s:s + P], m0 + v, c_mx, slice(j0 % J_HALF + s, j0 % J_HALF + s + P))
        out_view = out.rearrange("(m p) j -> p m j", p=P)
        for number, (j0, width, m0, bank) in enumerate(sums):
            per = BANK // width
            for v in range(per):
                fp8_pass(bank[:, v, :], wq, 1, m0 + v, x1[j0], slice(0, width), False, False)
                fp8_pass(bank[:, v, :], wr, 1, m0 + v, x1[j0], slice(0, width), False, v == per - 1)
            result = keep.tile([P, per, width], F32, name="result%d" % number)
            if number < BANKS_ON_SCALAR:
                for v in range(per):
                    nc.scalar.activation(out=result[:, v, :], in_=bank[:, v, :], func=IDENT, bias=bias[:, m0 + v:m0 + v + 1], scale=1.0)
            else:
                nc.vector.tensor_tensor(out=result[:], in0=bank[:], in1=bias[:, m0:m0 + per].unsqueeze(2).to_broadcast([P, per, width]), op=ADD)
            nc.sync.dma_start(out=out_view[:, m0:m0 + per, j0:j0 + width], in_=result[:])
